import numpy as np
import ml_dtypes


def mxq(x, axis, fmt="e4m3"):
    dtype, down = {"e4m3": (ml_dtypes.float8_e4m3fn, 7), "e5m2": (ml_dtypes.float8_e5m2, 14)}[fmt]
    v = np.moveaxis(np.asarray(x, np.float32).astype(ml_dtypes.bfloat16).astype(np.float64), axis, -1)
    blocks = v.reshape(v.shape[:-1] + (-1, 32))
    amax = np.abs(blocks).max(-1, keepdims=True)
    byte = np.maximum(np.where(amax > 0, np.frexp(amax)[1] - 1 + 127, 0) - down, 1)
    scale = np.exp2(byte - 127.0)
    codes = (blocks / scale).astype(np.float32).astype(dtype).astype(np.float64)
    return np.moveaxis((codes * scale).reshape(v.shape), -1, axis)


WIDE = False


def mx_kscale(k):
    if not WIDE:
        return np.ones(k)
    levels = np.array([10, -10, 5, -5, 0])
    if k % 512:
        return np.exp2(np.random.permutation(np.resize(levels, k // 32))).repeat(32)
    a = np.empty((k // 512, 16))
    for p in range(k // 512):
        a[p, :8] = np.random.permutation(np.resize(levels, 8))
        for g in range(8):
            far = levels[np.abs(levels - a[p, g]) >= 10]
            a[p, g + 8] = far[np.random.randint(len(far))]
    return np.exp2(a.ravel()).repeat(32)


def f64(x):
    return np.asarray(x).astype(np.float64)


def striped(idx):
    return np.tile(idx.reshape(-1, 16).T, (8, 1)).astype(np.uint16)


def unstriped(offs):
    return offs[:16].T.reshape(-1).astype(np.int64)


def pack_weight(w):
    k, n = w.shape
    w = f64(np.asarray(w, np.float32).astype(ml_dtypes.bfloat16)).reshape(k // 32, 32, n)
    amax = np.abs(w).max(1)
    byte = np.clip(np.where(amax > 0, np.frexp(amax)[1] - 1 + 127 - 7, 1), 1, 254)
    scaled = (w * np.exp2(127.0 - byte)[:, None, :]).reshape(k, n).astype(np.float32)
    words = np.ascontiguousarray(scaled.reshape(k // 512, 128, 4, n).transpose(0, 1, 3, 2)).astype(ml_dtypes.float8_e4m3fn).view(np.uint8)
    return words, np.ascontiguousarray(byte.astype(np.uint8).reshape(k // 512, 16, n))


def unpack_weight(words, scales):
    g, p, n, _ = words.shape
    vals = np.ascontiguousarray(words).view(ml_dtypes.float8_e4m3fn).astype(np.float64) * np.repeat(np.exp2(scales.astype(np.float64) - 127.0), 8, axis=1)[..., None]
    return vals.transpose(0, 1, 3, 2).reshape(g * 512, n)


K, T, S, N, D = 512, 2048, 512, 256, 3
P = 2 ** 7


def setup_inputs():
    n = np.random.standard_normal
    s = mx_kscale(K)[:, None]
    packed_xT = pack_weight(n((K, T)) * s)
    return {
        "x_words": packed_xT[0],
        "x_scales": packed_xT[1],
        "w1": (n((K, N)) / np.sqrt(K) / s).astype(np.float32),
        "w2": (n((K, N)) / np.sqrt(K) / s).astype(np.float32),
        "cpl": (np.tile(np.random.uniform(0.1, 0.7, (D, 1, S)), (1, P, 1))).astype(np.float32),
        "offs": striped(np.random.permutation(T)[:S]),
        "pos1": striped(np.random.permutation(S)[:S]),
        "pos2": striped(np.random.permutation(S)[:S]),
        "pos3": striped(np.random.permutation(S)[:S]),
    }


def reference(x_words, x_scales, w1, w2, cpl, offs, pos1, pos2, pos3):
    xq = unpack_weight(x_words, x_scales)[:, unstriped(offs)]
    y = mxq(f64(w1), 0, "e4m3").T @ xq
    z = mxq(f64(w2), 0, "e4m3").T @ xq
    rr = np.sqrt((y) ** 2 + (z) ** 2 + 0.1)
    cs = y / rr
    mc = cs[:, unstriped(pos1)] * f64(cpl)[0, :1] + cs[:, unstriped(pos2)] * f64(cpl)[1, :1] + cs[:, unstriped(pos3)] * f64(cpl)[2, :1]
    sn = z / rr
    msn = sn[:, unstriped(pos1)] * f64(cpl)[0, :1] + sn[:, unstriped(pos2)] * f64(cpl)[1, :1] + sn[:, unstriped(pos3)] * f64(cpl)[2, :1]
    tq = cs * msn - (sn * mc)
    return np.sqrt((mc) ** 2 + (msn) ** 2 + 0.02) - (0.5 * ((tq) ** 2))

@@ -1,0 +1,192 @@
+from contextlib import ExitStack
+import math
+
+import concourse.mybir as mybir
+from concourse.masks import make_identity
+
+K, T, S, N, D = 512, 2048, 512, 256, 3
+P = 128
+HALF = S // 2
+FLOPS = 2 * 2 * K * N * S
+
+F32 = mybir.dt.float32
+BF16 = mybir.dt.bfloat16
+I32 = mybir.dt.int32
+U32 = mybir.dt.uint32
+U16 = mybir.dt.uint16
+U8 = mybir.dt.uint8
+FP8X4 = mybir.dt.float8_e4m3fn_x4
+ACT = mybir.ActivationFunctionType
+ALU = mybir.AluOpType
+
+
+def tile_picked_yphas_order_p_kernel(tc, x_words, x_scales, w1, w2, cpl, offs, pos1, pos2, pos3, out):
+    nc = tc.nc
+    with ExitStack() as ctx:
+        keep = ctx.enter_context(tc.tile_pool(name="keep", bufs=1))
+        work = ctx.enter_context(tc.tile_pool(name="work", bufs=2))
+        prods = ctx.enter_context(tc.tile_pool(name="prods", bufs=6))
+        psum = ctx.enter_context(tc.psum_pool(name="psum", bufs=2))
+
+        offs_sb = keep.tile([P, S // 16], U16, name="offs_sb")
+        pos_sb = [keep.tile([P, S // 16], U16, name=f"pos_sb{d}") for d in range(D)]
+        words_all = keep.tile([P, T], U32, name="words_all", align_bytes=64)
+        scales_all = keep.tile([P, T], U8, name="scales_all", align_bytes=64)
+        w_raw = [[keep.tile([P, 4, P], F32, name=f"w_raw{b}{i}") for i in range(2)] for b in range(2)]
+        coupling = [keep.tile([P, S], F32, name=f"coupling{d}") for d in range(D)]
+        ident = keep.tile([P, P], F32, name="ident")
+
+        def load_weights(b):
+            for i, w in enumerate((w1, w2)):
+                nc.sync.dma_start(out=w_raw[b][i][:], in_=w[:, b * P:(b + 1) * P].rearrange("(p j) n -> p j n", j=4))
+
+        nc.vector.memset(scales_all[:].bitcast(I32), 0)
+        for q in range(4):
+            nc.scalar.dma_start(out=scales_all[32 * q:32 * q + 4, :].bitcast(I32), in_=x_scales[0, 4 * q:4 * q + 4, :].bitcast(I32))
+        nc.sync.dma_start(out=offs_sb[:], in_=offs)
+        nc.sync.dma_start(out=words_all[:].bitcast(I32), in_=x_words[0].rearrange("p n t -> p (n t)").bitcast(I32))
+        load_weights(0)
+        nc.sync.dma_start(out=pos_sb[0][:], in_=pos1)
+        nc.sync.dma_start(out=coupling[0][:], in_=cpl[0])
+        load_weights(1)
+        nc.sync.dma_start(out=pos_sb[1][:], in_=pos2)
+        nc.sync.dma_start(out=coupling[1][:], in_=cpl[1])
+        nc.sync.dma_start(out=pos_sb[2][:], in_=pos3)
+        nc.sync.dma_start(out=coupling[2][:], in_=cpl[2])
+        make_identity(nc, ident[:])
+
+        x_sc = keep.tile([P, S], U8, name="x_sc", align_bytes=64)
+        x_cd = keep.tile([P, S], U32, name="x_cd", align_bytes=64)
+        nc.vector.tensor_copy(out=x_sc[:], in_=scales_all[:].indirect(offs_sb[:]))
+        nc.vector.tensor_copy(out=x_cd[:], in_=words_all[:].indirect(offs_sb[:]))
+
+        def quantize(b, i):
+            grouped = keep.tile([P, P, 4], BF16, name=f"grouped{b}{i}", align_bytes=64)
+            nc.scalar.copy(
+                out=grouped[:].rearrange("p (c i) t -> p c t i", i=4),
+                in_=w_raw[b][i][:].rearrange("p t (c i) -> p c t i", i=4))
+            codes = keep.tile([P, P], U32, name=f"codes{b}{i}", align_bytes=64)
+            scales = keep.tile([P, P], U8, name=f"scales{b}{i}", align_bytes=64)
+            nc.vector.quantize_mx(out=codes[:].bitcast(FP8X4), scales=scales[:], in_=grouped[:].rearrange("p c t -> p (c t)"))
+            return codes, scales
+
+        def multiply(quantized):
+            yz = [psum.tile([P, 2, HALF], F32, name="yz") for h in range(2)]
+            sq = [work.tile([P, 2, HALF], F32, name="sq") for h in range(2)]
+            for i in range(2):
+                codes, scales = quantized[i]
+                for h in range(2):
+                    cols = slice(h * HALF, (h + 1) * HALF)
+                    nc.tensor.matmul_mx(out=yz[h][:, i, :], lhsT=codes[:].bitcast(FP8X4), lhsT_scale=scales[:],
+                                        rhs=x_cd[:, cols].bitcast(FP8X4), rhs_scale=x_sc[:, cols], start=True, stop=True)
+                    nc.scalar.activation(out=sq[h][:, i, :], in_=yz[h][:, i, :], func=ACT.Square)
+            return yz, sq
+
+        def inverse_radius(sq):
+            inv = []
+            for h in range(2):
+                rr2 = work.tile([P, HALF], F32, name="rr2")
+                nc.vector.tensor_tensor(out=rr2[:], in0=sq[h][:, 0, :], in1=sq[h][:, 1, :], op=ALU.add)
+                inv_rr = work.tile([P, HALF], F32, name="inv_rr")
+                nc.scalar.activation(out=inv_rr[:], in_=rr2[:], func=ACT.Abs_reciprocal_sqrt, bias=0.1)
+                inv.append(inv_rr)
+            return inv
+
+        def normalise(b, yz, inv):
+            cs = keep.tile([P, S], F32, name=f"cs{b}")
+            sn = keep.tile([P, S], F32, name=f"sn{b}")
+            for i, dst in ((1, sn), (0, cs)):
+                for h in range(2):
+                    nc.vector.tensor_tensor(out=dst[:, h * HALF:(h + 1) * HALF], in0=yz[h][:, i, :], in1=inv[h][:], op=ALU.mult)
+            u_t = keep.tile([P, 4, 2, P], F32, name=f"u_t{b}")
+            for i, (src, sign) in enumerate(((cs, 1.0), (sn, -1.0))):
+                bank = psum.tile([P, 4, P], F32, name="u_bank")
+                for jb in range(4):
+                    nc.tensor.transpose(bank[:, jb, :], src[:, jb * P:(jb + 1) * P], ident[:])
+                nc.scalar.activation(out=u_t[:, :, i, :], in_=bank[:], func=ACT.Copy, scale=sign * math.sqrt(0.5))
+            return (sn, cs), u_t
+
+        def add_turned(dst, terms):
+            for n, term in enumerate(terms):
+                nc.tensor.matmul(dst, lhsT=term, rhs=ident[:], start=(n == 0), stop=(n == len(terms) - 1), is_transpose=True)
+
+        def neighbour_mean(dst, window, first, count):
+            terms = []
+            for d in range(D):
+                term = prods.tile([P, count * P], F32, name="term")
+                nc.vector.tensor_tensor(out=term[:], in0=window[:].indirect(pos_sb[d][:, first * 8:(first + count) * 8]),
+                                        in1=coupling[d][:, first * P:(first + count) * P], op=ALU.mult)
+                terms.append(term)
+            for jb in range(count):
+                add_turned(dst[jb], [term[:, jb * P:(jb + 1) * P] for term in terms])
+
+        def products(u_t, first, count, mean_t):
+            cross = work.tile([P, count, 2, P], F32, name="cross")
+            nc.vector.tensor_tensor(out=cross[:], in0=mean_t[:], in1=u_t[:, first:first + count, :, :], op=ALU.mult)
+            mean_sq = work.tile([P, count, 2, P], F32, name="mean_sq")
+            nc.scalar.activation(out=mean_sq[:], in_=mean_t[:], func=ACT.Square)
+            sums = psum.tile([P, 2, count, P], F32, name="sums")
+            for i, src in enumerate((cross, mean_sq)):
+                for jb in range(count):
+                    add_turned(sums[:, i, jb, :], [src[:, jb, 0, :], src[:, jb, 1, :]])
+            torque = work.tile([P, count * P], F32, name="torque")
+            nc.scalar.activation(out=torque[:], in_=sums[:, 0, :, :].rearrange("p a m -> p (a m)"), func=ACT.Square)
+            order = work.tile([P, count * P], F32, name="order")
+            nc.scalar.activation(out=order[:], in_=sums[:, 1, :, :].rearrange("p a m -> p (a m)"), func=ACT.Sqrt, bias=0.02)
+            return order, torque
+
+        def finish(b, first, count, order, torque):
+            result = work.tile([P, count * P], F32, name="result")
+            nc.vector.tensor_tensor(out=result[:], in0=order[:], in1=torque[:], op=ALU.subtract)
+            nc.sync.dma_start(out=out[b * P:(b + 1) * P, first * P:(first + count) * P], in_=result[:])
+
+        quantized = [[quantize(b, i) for i in range(2)] for b in range(1)]
+        yz0, sq0 = multiply(quantized[0])
+        quantized.append([quantize(1, i) for i in range(2)])
+        blocks = [normalise(0, yz0, inverse_radius(sq0))]
+        yz1, sq1 = multiply(quantized[1])
+
+        units = [(0, 0, 2), (0, 2, 2), (1, 0, 2), (1, 2, 1)]
+        means = []
+        parts = []
+        for step, (b, first, count) in enumerate(units):
+            windows = blocks[b][0]
+            mean_t = psum.tile([P, count, 2, P], F32, name="mean_t")
+            means.append(mean_t)
+            neighbour_mean([mean_t[:, jb, 0, :] for jb in range(count)], windows[0], first, count)
+            if step == 0:
+                inv1 = inverse_radius(sq1)
+            if step >= 2:
+                finish(*units[step - 2], *parts[step - 2])
+            if step >= 1:
+                pb, pfirst, pcount = units[step - 1]
+                parts.append(products(blocks[pb][1], pfirst, pcount, means[step - 1]))
+            neighbour_mean([mean_t[:, jb, 1, :] for jb in range(count)], windows[1], first, count)
+            if step == 0:
+                blocks.append(normalise(1, yz1, inv1))
+
+        windows, u_t = blocks[1]
+        radius = psum.tile([P, P], F32, name="u_bank")
+        twist = psum.tile([P, P], F32, name="u_bank")
+        mean_one = [psum.tile([P, P], F32, name="yz") for i in range(2)]
+
+        def last_products(i):
+            cross = work.tile([P, P], F32, name="cross_one")
+            nc.vector.tensor_tensor(out=cross[:], in0=mean_one[i][:], in1=u_t[:, 3, i, :], op=ALU.mult)
+            mean_sq = work.tile([P, P], F32, name="mean_sq_one")
+            nc.scalar.activation(out=mean_sq[:], in_=mean_one[i][:], func=ACT.Square)
+            for dst, src in ((twist, cross), (radius, mean_sq)):
+                nc.tensor.matmul(dst[:], lhsT=src[:], rhs=ident[:], start=(i == 0), stop=(i == 1), is_transpose=True)
+
+        neighbour_mean([mean_one[0][:]], windows[0], 3, 1)
+        parts.append(products(u_t, 2, 1, means[3]))
+        finish(*units[2], *parts[2])
+        neighbour_mean([mean_one[1][:]], windows[1], 3, 1)
+        last_products(0)
+        finish(*units[3], *parts[3])
+        last_products(1)
+        torque = work.tile([P, P], F32, name="torque")
+        nc.scalar.activation(out=torque[:], in_=twist[:], func=ACT.Square)
+        order = work.tile([P, P], F32, name="order")
+        nc.scalar.activation(out=order[:], in_=radius[:], func=ACT.Sqrt, bias=0.02)
+        finish(1, 3, 1, order, torque)

@@ -26,167 +26,186 @@ def tile_picked_yphas_order_p_kernel(tc, x_words, x_scales, w1, w2, cpl, offs, p
         keep = ctx.enter_context(tc.tile_pool(name="keep", bufs=1))
         work = ctx.enter_context(tc.tile_pool(name="work", bufs=2))
         prods = ctx.enter_context(tc.tile_pool(name="prods", bufs=6))
+        slots = ctx.enter_context(tc.tile_pool(name="slots", bufs=1))
         psum = ctx.enter_context(tc.psum_pool(name="psum", bufs=2))
+        single = ctx.enter_context(tc.psum_pool(name="single", bufs=1))
 
         offs_sb = keep.tile([P, S // 16], U16, name="offs_sb")
         pos_sb = [keep.tile([P, S // 16], U16, name=f"pos_sb{d}") for d in range(D)]
-        words_all = keep.tile([P, T], U32, name="words_all", align_bytes=64)
         scales_all = keep.tile([P, T], U8, name="scales_all", align_bytes=64)
-        w_raw = [[keep.tile([P, 4, P], F32, name=f"w_raw{b}{i}") for i in range(2)] for b in range(2)]
-        coupling = [keep.tile([P, S], F32, name=f"coupling{d}") for d in range(D)]
         ident = keep.tile([P, P], F32, name="ident")
-
-        def load_weights(b):
-            for i, w in enumerate((w1, w2)):
-                nc.sync.dma_start(out=w_raw[b][i][:], in_=w[:, b * P:(b + 1) * P].rearrange("(p j) n -> p j n", j=4))
-
         nc.vector.memset(scales_all[:].bitcast(I32), 0)
-        for q in range(4):
-            nc.scalar.dma_start(out=scales_all[32 * q:32 * q + 4, :].bitcast(I32), in_=x_scales[0, 4 * q:4 * q + 4, :].bitcast(I32))
-        nc.sync.dma_start(out=offs_sb[:], in_=offs)
-        nc.sync.dma_start(out=words_all[:].bitcast(I32), in_=x_words[0].rearrange("p n t -> p (n t)").bitcast(I32))
-        load_weights(0)
-        nc.sync.dma_start(out=pos_sb[0][:], in_=pos1)
-        nc.sync.dma_start(out=coupling[0][:], in_=cpl[0])
-        load_weights(1)
-        nc.sync.dma_start(out=pos_sb[1][:], in_=pos2)
-        nc.sync.dma_start(out=coupling[1][:], in_=cpl[1])
-        nc.sync.dma_start(out=pos_sb[2][:], in_=pos3)
-        nc.sync.dma_start(out=coupling[2][:], in_=cpl[2])
+        warm_in = slots.tile([P, 1], F32, name="warm_in", tag="words", align_bytes=64)
+        warm_out = keep.tile([P, 1], F32, name="warm_out")
+        nc.vector.memset(warm_in[:], 1.0)
+        nc.scalar.activation(out=warm_out[:], in_=warm_in[:], func=ACT.Abs_reciprocal_sqrt)
         make_identity(nc, ident[:])
+        words_all = slots.tile([P, T], U32, name="words_all", tag="words", align_bytes=64)
+
+        def load_weights(b, tiles):
+            for w, raw in zip((w1, w2), tiles):
+                nc.sync.dma_start(out=raw, in_=w[:, b * P:(b + 1) * P].rearrange("(p j) n -> p j n", j=4))
+
+        for dst, src in zip([offs_sb] + pos_sb, (offs, pos1, pos2, pos3)):
+            nc.sync.dma_start(out=dst[:], in_=src)
+        w_raw = [[slots.tile([P, 4, P], F32, name=f"w_raw{i}", tag=f"raw{i}")[:] for i in range(2)]]
+        load_weights(0, w_raw[0])
+        for q in range(4):
+            nc.sync.dma_start(out=scales_all[32 * q:32 * q + 4, :].bitcast(I32), in_=x_scales[0, 4 * q:4 * q + 4, :].bitcast(I32))
+        nc.sync.dma_start(out=words_all[:].bitcast(I32), in_=x_words[0].rearrange("p n t -> p (n t)").bitcast(I32))
+
+        def quantize(raws, tag):
+            width = len(raws) * P
+            grouped = slots.tile([P, width, 4], BF16, name="grouped", tag=tag, align_bytes=64)
+            for n, raw in enumerate(raws):
+                nc.scalar.copy(out=grouped[:, n * P:(n + 1) * P, :].rearrange("p (c i) t -> p c t i", i=4),
+                               in_=raw.rearrange("p t (c i) -> p c t i", i=4))
+            codes = keep.tile([P, width], U32, name=f"codes_{tag}", align_bytes=64)
+            scales = keep.tile([P, width], U8, name=f"scales_{tag}", align_bytes=64)
+            nc.vector.quantize_mx(out=codes[:].bitcast(FP8X4), scales=scales[:], in_=grouped[:].rearrange("p c t -> p (c t)"))
+            return [(codes[:, n * P:(n + 1) * P], scales[:, n * P:(n + 1) * P]) for n in range(len(raws))]
 
         x_sc = keep.tile([P, S], U8, name="x_sc", align_bytes=64)
         x_cd = keep.tile([P, S], U32, name="x_cd", align_bytes=64)
         nc.vector.tensor_copy(out=x_sc[:], in_=scales_all[:].indirect(offs_sb[:]))
-        nc.vector.tensor_copy(out=x_cd[:], in_=words_all[:].indirect(offs_sb[:]))
+        quantized0 = [quantize([w_raw[0][i]], f"first{i}")[0] for i in range(2)]
+        coupling = [slots.tile([P, S], F32, name="coupling0", tag="raw0"), slots.tile([P, S], F32, name="coupling1", tag="raw1"),
+                    slots.tile([P, S], F32, name="coupling2", tag="first0", align_bytes=64)]
+        for d in range(D):
+            nc.sync.dma_start(out=coupling[d][:], in_=cpl[d])
+        w_late = slots.tile([P, 2, 4, P], F32, name="w_late", tag="first1", align_bytes=64)
+        w_raw.append([w_late[:, i, :, :] for i in range(2)])
+        load_weights(1, w_raw[1])
+        for h in range(2):
+            nc.vector.tensor_copy(out=x_cd[:, h * HALF:(h + 1) * HALF], in_=words_all[:].indirect(offs_sb[:, h * 16:(h + 1) * 16]))
 
-        def quantize(b, i):
-            grouped = keep.tile([P, P, 4], BF16, name=f"grouped{b}{i}", align_bytes=64)
-            nc.scalar.copy(
-                out=grouped[:].rearrange("p (c i) t -> p c t i", i=4),
-                in_=w_raw[b][i][:].rearrange("p t (c i) -> p c t i", i=4))
-            codes = keep.tile([P, P], U32, name=f"codes{b}{i}", align_bytes=64)
-            scales = keep.tile([P, P], U8, name=f"scales{b}{i}", align_bytes=64)
-            nc.vector.quantize_mx(out=codes[:].bitcast(FP8X4), scales=scales[:], in_=grouped[:].rearrange("p c t -> p (c t)"))
-            return codes, scales
+        def product(dst, weights, cols):
+            codes, scales = weights
+            nc.tensor.matmul_mx(out=dst, lhsT=codes.bitcast(FP8X4), lhsT_scale=scales,
+                                rhs=x_cd[:, cols].bitcast(FP8X4), rhs_scale=x_sc[:, cols], start=True, stop=True)
 
-        def multiply(quantized):
-            yz = [psum.tile([P, 2, HALF], F32, name="yz") for h in range(2)]
-            sq = [work.tile([P, 2, HALF], F32, name="sq") for h in range(2)]
-            for i in range(2):
-                codes, scales = quantized[i]
-                for h in range(2):
-                    cols = slice(h * HALF, (h + 1) * HALF)
-                    nc.tensor.matmul_mx(out=yz[h][:, i, :], lhsT=codes[:].bitcast(FP8X4), lhsT_scale=scales[:],
-                                        rhs=x_cd[:, cols].bitcast(FP8X4), rhs_scale=x_sc[:, cols], start=True, stop=True)
-                    nc.scalar.activation(out=sq[h][:, i, :], in_=yz[h][:, i, :], func=ACT.Square)
-            return yz, sq
+        def inverse_radius(sq, width, tag):
+            rr2 = slots.tile([P, width], F32, name="rr2", tag=tag, align_bytes=64)
+            nc.vector.tensor_tensor(out=rr2[:], in0=sq[:, 0, :], in1=sq[:, 1, :], op=ALU.add)
+            inv_rr = keep.tile([P, width], F32, name=f"inv_{tag}")
+            nc.scalar.activation(out=inv_rr[:], in_=rr2[:], func=ACT.Abs_reciprocal_sqrt, bias=0.1)
+            return inv_rr
 
-        def inverse_radius(sq):
-            inv = []
-            for h in range(2):
-                rr2 = work.tile([P, HALF], F32, name="rr2")
-                nc.vector.tensor_tensor(out=rr2[:], in0=sq[h][:, 0, :], in1=sq[h][:, 1, :], op=ALU.add)
-                inv_rr = work.tile([P, HALF], F32, name="inv_rr")
-                nc.scalar.activation(out=inv_rr[:], in_=rr2[:], func=ACT.Abs_reciprocal_sqrt, bias=0.1)
-                inv.append(inv_rr)
-            return inv
-
-        def normalise(b, yz, inv):
+        def normalise(b, pieces):
             cs = keep.tile([P, S], F32, name=f"cs{b}")
             sn = keep.tile([P, S], F32, name=f"sn{b}")
             for i, dst in ((1, sn), (0, cs)):
-                for h in range(2):
-                    nc.vector.tensor_tensor(out=dst[:, h * HALF:(h + 1) * HALF], in0=yz[h][:, i, :], in1=inv[h][:], op=ALU.mult)
-            u_t = keep.tile([P, 4, 2, P], F32, name=f"u_t{b}")
+                for cols, yz, inv in pieces:
+                    nc.vector.tensor_tensor(out=dst[:, cols], in0=yz[i], in1=inv[:], op=ALU.mult)
+            u_t = keep.tile([P, 2, 4, P], F32, name=f"u_t{b}")
             for i, (src, sign) in enumerate(((cs, 1.0), (sn, -1.0))):
-                bank = psum.tile([P, 4, P], F32, name="u_bank")
+                bank = single.tile([P, 4, P], F32, name="u_bank", tag=("twist", "radius")[i])
                 for jb in range(4):
                     nc.tensor.transpose(bank[:, jb, :], src[:, jb * P:(jb + 1) * P], ident[:])
-                nc.scalar.activation(out=u_t[:, :, i, :], in_=bank[:], func=ACT.Copy, scale=sign * math.sqrt(0.5))
+                nc.scalar.activation(out=u_t[:, i, :, :], in_=bank[:], func=ACT.Copy, scale=sign * math.sqrt(0.5))
             return (sn, cs), u_t
 
         def add_turned(dst, terms):
             for n, term in enumerate(terms):
                 nc.tensor.matmul(dst, lhsT=term, rhs=ident[:], start=(n == 0), stop=(n == len(terms) - 1), is_transpose=True)
 
-        def neighbour_mean(dst, window, first, count):
+        def neighbour_mean(dst, window, first, count, homes=()):
             terms = []
             for d in range(D):
-                term = prods.tile([P, count * P], F32, name="term")
-                nc.vector.tensor_tensor(out=term[:], in0=window[:].indirect(pos_sb[d][:, first * 8:(first + count) * 8]),
+                term = homes[d][:, 0:count * P] if d < len(homes) else prods.tile([P, count * P], F32, name="term")[:]
+                nc.vector.tensor_tensor(out=term, in0=window[:].indirect(pos_sb[d][:, first * 8:(first + count) * 8]),
                                         in1=coupling[d][:, first * P:(first + count) * P], op=ALU.mult)
                 terms.append(term)
             for jb in range(count):
                 add_turned(dst[jb], [term[:, jb * P:(jb + 1) * P] for term in terms])
 
-        def products(u_t, first, count, mean_t):
-            cross = work.tile([P, count, 2, P], F32, name="cross")
-            nc.vector.tensor_tensor(out=cross[:], in0=mean_t[:], in1=u_t[:, first:first + count, :, :], op=ALU.mult)
-            mean_sq = work.tile([P, count, 2, P], F32, name="mean_sq")
+        def products(mean_t, u_t, i, first, count):
+            cross = work.tile([P, count, P], F32, name=f"cross{i}")
+            nc.vector.tensor_tensor(out=cross[:], in0=mean_t[:], in1=u_t[:, i, first:first + count, :], op=ALU.mult)
+            mean_sq = work.tile([P, count, P], F32, name=f"mean_sq{i}")
             nc.scalar.activation(out=mean_sq[:], in_=mean_t[:], func=ACT.Square)
-            sums = psum.tile([P, 2, count, P], F32, name="sums")
-            for i, src in enumerate((cross, mean_sq)):
+            return cross, mean_sq
+
+        def activate(twist, radius, count):
+            torque = keep.tile([P, count * P], F32, name=f"torque{len(parts)}")
+            nc.scalar.activation(out=torque[:], in_=twist[:].rearrange("p a m -> p (a m)"), func=ACT.Square)
+            order = keep.tile([P, count * P], F32, name=f"order{len(parts)}")
+            nc.scalar.activation(out=order[:], in_=radius[:].rearrange("p a m -> p (a m)"), func=ACT.Sqrt, bias=0.02)
+            parts.append((order, torque))
+
+        def turn_back(pair, count):
+            banks = [single.tile([P, count, P], F32, name=tag, tag=tag) for tag in ("twist", "radius")]
+            for n, bank in enumerate(banks):
                 for jb in range(count):
-                    add_turned(sums[:, i, jb, :], [src[:, jb, 0, :], src[:, jb, 1, :]])
-            torque = work.tile([P, count * P], F32, name="torque")
-            nc.scalar.activation(out=torque[:], in_=sums[:, 0, :, :].rearrange("p a m -> p (a m)"), func=ACT.Square)
-            order = work.tile([P, count * P], F32, name="order")
-            nc.scalar.activation(out=order[:], in_=sums[:, 1, :, :].rearrange("p a m -> p (a m)"), func=ACT.Sqrt, bias=0.02)
-            return order, torque
+                    add_turned(bank[:, jb, :], [pair[0][n][:, jb, :], pair[1][n][:, jb, :]])
+            activate(*banks, count)
 
-        def finish(b, first, count, order, torque):
-            result = work.tile([P, count * P], F32, name="result")
-            nc.vector.tensor_tensor(out=result[:], in0=order[:], in1=torque[:], op=ALU.subtract)
-            nc.sync.dma_start(out=out[b * P:(b + 1) * P, first * P:(first + count) * P], in_=result[:])
+        def finish(u, result):
+            b, first, count = units[u]
+            order, torque = parts[u]
+            nc.vector.tensor_tensor(out=result, in0=order[:], in1=torque[:], op=ALU.subtract)
+            nc.sync.dma_start(out=out[b * P:(b + 1) * P, first * P:(first + count) * P], in_=result)
 
-        quantized = [[quantize(b, i) for i in range(2)] for b in range(1)]
-        yz0, sq0 = multiply(quantized[0])
-        quantized.append([quantize(1, i) for i in range(2)])
-        blocks = [normalise(0, yz0, inverse_radius(sq0))]
-        yz1, sq1 = multiply(quantized[1])
+        pieces = []
+        for h in range(2):
+            cols = slice(h * HALF, (h + 1) * HALF)
+            yz = psum.tile([P, 2, HALF], F32, name="yz")
+            for i in range(2):
+                product(yz[:, i, :], quantized0[i], cols)
+            sq = keep.tile([P, 2, HALF], F32, name=f"sq0{h}")
+            nc.scalar.activation(out=sq[:], in_=yz[:], func=ACT.Square)
+            pieces.append((cols, [yz[:, 0, :], yz[:, 1, :]], sq))
+        blocks = [normalise(0, [(cols, yz, inverse_radius(sq, HALF, ("rr2a", "reused")[h])) for h, (cols, yz, sq) in enumerate(pieces)])]
 
-        units = [(0, 0, 2), (0, 2, 2), (1, 0, 2), (1, 2, 1)]
+        units = [(0, 0, 2), (0, 2, 2), (1, 0, 2), (1, 2, 1), (1, 3, 1)]
+        stages = [(u, i) for u in range(len(units)) for i in range(2)]
+        last = len(units) - 1
         means = []
+        made = []
         parts = []
-        for step, (b, first, count) in enumerate(units):
-            windows = blocks[b][0]
-            mean_t = psum.tile([P, count, 2, P], F32, name="mean_t")
-            means.append(mean_t)
-            neighbour_mean([mean_t[:, jb, 0, :] for jb in range(count)], windows[0], first, count)
-            if step == 0:
-                inv1 = inverse_radius(sq1)
-            if step >= 2:
-                finish(*units[step - 2], *parts[step - 2])
-            if step >= 1:
-                pb, pfirst, pcount = units[step - 1]
-                parts.append(products(blocks[pb][1], pfirst, pcount, means[step - 1]))
-            neighbour_mean([mean_t[:, jb, 1, :] for jb in range(count)], windows[1], first, count)
-            if step == 0:
-                blocks.append(normalise(1, yz1, inv1))
-
-        windows, u_t = blocks[1]
-        radius = psum.tile([P, P], F32, name="u_bank")
-        twist = psum.tile([P, P], F32, name="u_bank")
-        mean_one = [psum.tile([P, P], F32, name="yz") for i in range(2)]
-
-        def last_products(i):
-            cross = work.tile([P, P], F32, name="cross_one")
-            nc.vector.tensor_tensor(out=cross[:], in0=mean_one[i][:], in1=u_t[:, 3, i, :], op=ALU.mult)
-            mean_sq = work.tile([P, P], F32, name="mean_sq_one")
-            nc.scalar.activation(out=mean_sq[:], in_=mean_one[i][:], func=ACT.Square)
-            for dst, src in ((twist, cross), (radius, mean_sq)):
-                nc.tensor.matmul(dst[:], lhsT=src[:], rhs=ident[:], start=(i == 0), stop=(i == 1), is_transpose=True)
-
-        neighbour_mean([mean_one[0][:]], windows[0], 3, 1)
-        parts.append(products(u_t, 2, 1, means[3]))
-        finish(*units[2], *parts[2])
-        neighbour_mean([mean_one[1][:]], windows[1], 3, 1)
-        last_products(0)
-        finish(*units[3], *parts[3])
-        last_products(1)
-        torque = work.tile([P, P], F32, name="torque")
-        nc.scalar.activation(out=torque[:], in_=twist[:], func=ACT.Square)
-        order = work.tile([P, P], F32, name="order")
-        nc.scalar.activation(out=order[:], in_=radius[:], func=ACT.Sqrt, bias=0.02)
-        finish(1, 3, 1, order, torque)
+        homes = []
+        for e in range(len(stages) + 1):
+            if e < len(stages):
+                u, i = stages[e]
+                b, first, count = units[u]
+                mean_t = psum.tile([P, count, P], F32, name="mean_t")
+                means.append(mean_t)
+                neighbour_mean([mean_t[:, jb, :] for jb in range(count)], blocks[b][0][i], first, count, homes)
+            homes = []
+            if e == 0:
+                quantized1 = quantize(w_raw[1], "reused")
+                yz1 = [psum.tile([P, S], F32, name="yz") for n in range(2)]
+                sq1 = keep.tile([P, 2, S], F32, name="sq1")
+                for n in range(2):
+                    product(yz1[n][:], quantized1[n], slice(0, S))
+                    nc.scalar.activation(out=sq1[:, n, :], in_=yz1[n][:], func=ACT.Square)
+                early = slots.tile([P, 2, HALF], F32, name="early", tag="reused", align_bytes=64)
+                homes = [early[:, 0, :], early[:, 1, :]]
+            if e >= 1:
+                u, i = stages[e - 1]
+                b, first, count = units[u]
+                made.append(products(means[e - 1], blocks[b][1], i, first, count))
+                if u == last:
+                    if i == 0:
+                        last_banks = [single.tile([P, 1, P], F32, name=tag) for tag in ("last_twist", "last_radius")]
+                    for n in range(2):
+                        nc.tensor.matmul(last_banks[n][:, 0, :], lhsT=made[-1][n][:, 0, :], rhs=ident[:],
+                                         start=(i == 0), stop=(i == 1), is_transpose=True)
+                    if i == 1:
+                        activate(*last_banks, 1)
+                elif i == 1:
+                    turn_back(made[-2:], count)
+            if e == 1:
+                inv1 = inverse_radius(sq1, S, "rr2b")
+                homes = [sq1[:, 0, 0:HALF], sq1[:, 1, 0:HALF]]
+            if e == 2:
+                blocks.append(normalise(1, [(slice(0, S), [yz1[0][:], yz1[1][:]], inv1)]))
+            if e == 4:
+                finish(0, sq1[:, 0, HALF:S])
+                homes = [parts[0][1][:]]
+            if e == len(stages) - 1:
+                spent = blocks[1][0][1]
+                finish(1, spent[:, 0:HALF])
+                finish(2, spent[:, HALF:S])
+                finish(3, sq1[:, 1, HALF:HALF + P])
+        finish(last, sq1[:, 1, HALF + P:S])

@@ -99,7 +99,7 @@ def tile_picked_yphas_order_p_kernel(tc, x_words, x_scales, w1, w2, cpl, offs, p
                     nc.vector.tensor_tensor(out=dst[:, cols], in0=yz[i], in1=inv[:], op=ALU.mult)
             u_t = keep.tile([P, 2, 4, P], F32, name=f"u_t{b}")
             for i, (src, sign) in enumerate(((cs, 1.0), (sn, -1.0))):
-                bank = single.tile([P, 4, P], F32, name="u_bank", tag=("twist", "radius")[i])
+                bank = single.tile([P, 4, P], F32, name="u_bank", tag=("twist", ("radius", "twist")[b])[i])
                 for jb in range(4):
                     nc.tensor.transpose(bank[:, jb, :], src[:, jb * P:(jb + 1) * P], ident[:])
                 nc.scalar.activation(out=u_t[:, i, :, :], in_=bank[:], func=ACT.Copy, scale=sign * math.sqrt(0.5))
@@ -197,14 +197,13 @@ def tile_picked_yphas_order_p_kernel(tc, x_words, x_scales, w1, w2, cpl, offs, p
                     turn_back(made[-2:], count)
             if e == 1:
                 inv1 = inverse_radius(sq1, S, "rr2b")
+                nc.scalar.activation(out=warm_out[:], in_=inv1[:, 0:1], func=ACT.Sqrt)
                 homes = [sq1[:, 0, 0:HALF], sq1[:, 1, 0:HALF]]
             if e == 2:
                 blocks.append(normalise(1, [(slice(0, S), [yz1[0][:], yz1[1][:]], inv1)]))
-            if e == 4:
-                finish(0, sq1[:, 0, HALF:S])
-                homes = [parts[0][1][:]]
             if e == len(stages) - 1:
                 spent = blocks[1][0][1]
+                finish(0, coupling[D - 1][:, HALF:S])
                 finish(1, spent[:, 0:HALF])
                 finish(2, spent[:, HALF:S])
                 finish(3, sq1[:, 1, HALF:HALF + P])

from contextlib import ExitStack
import math

import concourse.mybir as mybir
from concourse.masks import make_identity

K, T, S, N, D = 512, 2048, 512, 256, 3
P = 128
HALF = S // 2
FLOPS = 2 * 2 * K * N * S

F32 = mybir.dt.float32
BF16 = mybir.dt.bfloat16
I32 = mybir.dt.int32
U32 = mybir.dt.uint32
U16 = mybir.dt.uint16
U8 = mybir.dt.uint8
FP8X4 = mybir.dt.float8_e4m3fn_x4
ACT = mybir.ActivationFunctionType
ALU = mybir.AluOpType


def tile_picked_yphas_order_p_kernel(tc, x_words, x_scales, w1, w2, cpl, offs, pos1, pos2, pos3, out):
    nc = tc.nc
    with ExitStack() as ctx:
        keep = ctx.enter_context(tc.tile_pool(name="keep", bufs=1))
        work = ctx.enter_context(tc.tile_pool(name="work", bufs=2))
        prods = ctx.enter_context(tc.tile_pool(name="prods", bufs=6))
        slots = ctx.enter_context(tc.tile_pool(name="slots", bufs=1))
        psum = ctx.enter_context(tc.psum_pool(name="psum", bufs=2))
        single = ctx.enter_context(tc.psum_pool(name="single", bufs=1))

        offs_sb = keep.tile([P, S // 16], U16, name="offs_sb")
        pos_sb = [keep.tile([P, S // 16], U16, name=f"pos_sb{d}") for d in range(D)]
        scales_all = keep.tile([P, T], U8, name="scales_all", align_bytes=64)
        ident = keep.tile([P, P], F32, name="ident")
        nc.vector.memset(scales_all[:].bitcast(I32), 0)
        warm_in = slots.tile([P, 1], F32, name="warm_in", tag="words", align_bytes=64)
        warm_out = keep.tile([P, 1], F32, name="warm_out")
        nc.vector.memset(warm_in[:], 1.0)
        nc.scalar.activation(out=warm_out[:], in_=warm_in[:], func=ACT.Abs_reciprocal_sqrt)
        make_identity(nc, ident[:])
        words_all = slots.tile([P, T], U32, name="words_all", tag="words", align_bytes=64)

        def load_weights(b, tiles):
            for w, raw in zip((w1, w2), tiles):
                nc.sync.dma_start(out=raw, in_=w[:, b * P:(b + 1) * P].rearrange("(p j) n -> p j n", j=4))

        for dst, src in zip([offs_sb] + pos_sb, (offs, pos1, pos2, pos3)):
            nc.sync.dma_start(out=dst[:], in_=src)
        w_raw = [[slots.tile([P, 4, P], F32, name=f"w_raw{i}", tag=f"raw{i}")[:] for i in range(2)]]
        load_weights(0, w_raw[0])
        for q in range(4):
            nc.sync.dma_start(out=scales_all[32 * q:32 * q + 4, :].bitcast(I32), in_=x_scales[0, 4 * q:4 * q + 4, :].bitcast(I32))
        nc.sync.dma_start(out=words_all[:].bitcast(I32), in_=x_words[0].rearrange("p n t -> p (n t)").bitcast(I32))

        def quantize(raws, tag):
            width = len(raws) * P
            grouped = slots.tile([P, width, 4], BF16, name="grouped", tag=tag, align_bytes=64)
            for n, raw in enumerate(raws):
                nc.scalar.copy(out=grouped[:, n * P:(n + 1) * P, :].rearrange("p (c i) t -> p c t i", i=4),
                               in_=raw.rearrange("p t (c i) -> p c t i", i=4))
            codes = keep.tile([P, width], U32, name=f"codes_{tag}", align_bytes=64)
            scales = keep.tile([P, width], U8, name=f"scales_{tag}", align_bytes=64)
            nc.vector.quantize_mx(out=codes[:].bitcast(FP8X4), scales=scales[:], in_=grouped[:].rearrange("p c t -> p (c t)"))
            return [(codes[:, n * P:(n + 1) * P], scales[:, n * P:(n + 1) * P]) for n in range(len(raws))]

        x_sc = keep.tile([P, S], U8, name="x_sc", align_bytes=64)
        x_cd = keep.tile([P, S], U32, name="x_cd", align_bytes=64)
        nc.vector.tensor_copy(out=x_sc[:], in_=scales_all[:].indirect(offs_sb[:]))
        quantized0 = [quantize([w_raw[0][i]], f"first{i}")[0] for i in range(2)]
        coupling = [slots.tile([P, S], F32, name="coupling0", tag="raw0"), slots.tile([P, S], F32, name="coupling1", tag="raw1"),
                    slots.tile([P, S], F32, name="coupling2", tag="first0", align_bytes=64)]
        for d in range(D):
            nc.sync.dma_start(out=coupling[d][:], in_=cpl[d])
        w_late = slots.tile([P, 2, 4, P], F32, name="w_late", tag="first1", align_bytes=64)
        w_raw.append([w_late[:, i, :, :] for i in range(2)])
        load_weights(1, w_raw[1])
        for h in range(2):
            nc.vector.tensor_copy(out=x_cd[:, h * HALF:(h + 1) * HALF], in_=words_all[:].indirect(offs_sb[:, h * 16:(h + 1) * 16]))

        def product(dst, weights, cols):
            codes, scales = weights
            nc.tensor.matmul_mx(out=dst, lhsT=codes.bitcast(FP8X4), lhsT_scale=scales,
                                rhs=x_cd[:, cols].bitcast(FP8X4), rhs_scale=x_sc[:, cols], start=True, stop=True)

        def inverse_radius(sq, width, tag):
            rr2 = slots.tile([P, width], F32, name="rr2", tag=tag, align_bytes=64)
            nc.vector.tensor_tensor(out=rr2[:], in0=sq[:, 0, :], in1=sq[:, 1, :], op=ALU.add)
            inv_rr = keep.tile([P, width], F32, name=f"inv_{tag}")
            nc.scalar.activation(out=inv_rr[:], in_=rr2[:], func=ACT.Abs_reciprocal_sqrt, bias=0.1)
            return inv_rr

        def normalise(b, pieces):
            cs = keep.tile([P, S], F32, name=f"cs{b}")
            sn = keep.tile([P, S], F32, name=f"sn{b}")
            for i, dst in ((1, sn), (0, cs)):
                for cols, yz, inv in pieces:
                    nc.vector.tensor_tensor(out=dst[:, cols], in0=yz[i], in1=inv[:], op=ALU.mult)
            u_t = keep.tile([P, 2, 4, P], F32, name=f"u_t{b}")
            for i, (src, sign) in enumerate(((cs, 1.0), (sn, -1.0))):
                bank = single.tile([P, 4, P], F32, name="u_bank", tag=("twist", ("radius", "twist")[b])[i])
                for jb in range(4):
                    nc.tensor.transpose(bank[:, jb, :], src[:, jb * P:(jb + 1) * P], ident[:])
                nc.scalar.activation(out=u_t[:, i, :, :], in_=bank[:], func=ACT.Copy, scale=sign * math.sqrt(0.5))
            return (sn, cs), u_t

        def add_turned(dst, terms):
            for n, term in enumerate(terms):
                nc.tensor.matmul(dst, lhsT=term, rhs=ident[:], start=(n == 0), stop=(n == len(terms) - 1), is_transpose=True)

        def neighbour_mean(dst, window, first, count, homes=()):
            terms = []
            for d in range(D):
                term = homes[d][:, 0:count * P] if d < len(homes) else prods.tile([P, count * P], F32, name="term")[:]
                nc.vector.tensor_tensor(out=term, in0=window[:].indirect(pos_sb[d][:, first * 8:(first + count) * 8]),
                                        in1=coupling[d][:, first * P:(first + count) * P], op=ALU.mult)
                terms.append(term)
            for jb in range(count):
                add_turned(dst[jb], [term[:, jb * P:(jb + 1) * P] for term in terms])

        def products(mean_t, u_t, i, first, count):
            cross = work.tile([P, count, P], F32, name=f"cross{i}")
            nc.vector.tensor_tensor(out=cross[:], in0=mean_t[:], in1=u_t[:, i, first:first + count, :], op=ALU.mult)
            mean_sq = work.tile([P, count, P], F32, name=f"mean_sq{i}")
            nc.scalar.activation(out=mean_sq[:], in_=mean_t[:], func=ACT.Square)
            return cross, mean_sq

        def activate(twist, radius, count):
            torque = keep.tile([P, count * P], F32, name=f"torque{len(parts)}")
            nc.scalar.activation(out=torque[:], in_=twist[:].rearrange("p a m -> p (a m)"), func=ACT.Square)
            order = keep.tile([P, count * P], F32, name=f"order{len(parts)}")
            nc.scalar.activation(out=order[:], in_=radius[:].rearrange("p a m -> p (a m)"), func=ACT.Sqrt, bias=0.02)
            parts.append((order, torque))

        def turn_back(pair, count):
            banks = [single.tile([P, count, P], F32, name=tag, tag=tag) for tag in ("twist", "radius")]
            for n, bank in enumerate(banks):
                for jb in range(count):
                    add_turned(bank[:, jb, :], [pair[0][n][:, jb, :], pair[1][n][:, jb, :]])
            activate(*banks, count)

        def finish(u, result):
            b, first, count = units[u]
            order, torque = parts[u]
            nc.vector.tensor_tensor(out=result, in0=order[:], in1=torque[:], op=ALU.subtract)
            nc.sync.dma_start(out=out[b * P:(b + 1) * P, first * P:(first + count) * P], in_=result)

        pieces = []
        for h in range(2):
            cols = slice(h * HALF, (h + 1) * HALF)
            yz = psum.tile([P, 2, HALF], F32, name="yz")
            for i in range(2):
                product(yz[:, i, :], quantized0[i], cols)
            sq = keep.tile([P, 2, HALF], F32, name=f"sq0{h}")
            nc.scalar.activation(out=sq[:], in_=yz[:], func=ACT.Square)
            pieces.append((cols, [yz[:, 0, :], yz[:, 1, :]], sq))
        blocks = [normalise(0, [(cols, yz, inverse_radius(sq, HALF, ("rr2a", "reused")[h])) for h, (cols, yz, sq) in enumerate(pieces)])]

        units = [(0, 0, 2), (0, 2, 2), (1, 0, 2), (1, 2, 1), (1, 3, 1)]
        stages = [(u, i) for u in range(len(units)) for i in range(2)]
        last = len(units) - 1
        means = []
        made = []
        parts = []
        homes = []
        for e in range(len(stages) + 1):
            if e < len(stages):
                u, i = stages[e]
                b, first, count = units[u]
                mean_t = psum.tile([P, count, P], F32, name="mean_t")
                means.append(mean_t)
                neighbour_mean([mean_t[:, jb, :] for jb in range(count)], blocks[b][0][i], first, count, homes)
            homes = []
            if e == 0:
                quantized1 = quantize(w_raw[1], "reused")
                yz1 = [psum.tile([P, S], F32, name="yz") for n in range(2)]
                sq1 = keep.tile([P, 2, S], F32, name="sq1")
                for n in range(2):
                    product(yz1[n][:], quantized1[n], slice(0, S))
                    nc.scalar.activation(out=sq1[:, n, :], in_=yz1[n][:], func=ACT.Square)
                early = slots.tile([P, 2, HALF], F32, name="early", tag="reused", align_bytes=64)
                homes = [early[:, 0, :], early[:, 1, :]]
            if e >= 1:
                u, i = stages[e - 1]
                b, first, count = units[u]
                made.append(products(means[e - 1], blocks[b][1], i, first, count))
                if u == last:
                    if i == 0:
                        last_banks = [single.tile([P, 1, P], F32, name=tag) for tag in ("last_twist", "last_radius")]
                    for n in range(2):
                        nc.tensor.matmul(last_banks[n][:, 0, :], lhsT=made[-1][n][:, 0, :], rhs=ident[:],
                                         start=(i == 0), stop=(i == 1), is_transpose=True)
                    if i == 1:
                        activate(*last_banks, 1)
                elif i == 1:
                    turn_back(made[-2:], count)
            if e == 1:
                inv1 = inverse_radius(sq1, S, "rr2b")
                nc.scalar.activation(out=warm_out[:], in_=inv1[:, 0:1], func=ACT.Sqrt)
                homes = [sq1[:, 0, 0:HALF], sq1[:, 1, 0:HALF]]
            if e == 2:
                blocks.append(normalise(1, [(slice(0, S), [yz1[0][:], yz1[1][:]], inv1)]))
            if e == len(stages) - 1:
                spent = blocks[1][0][1]
                finish(0, coupling[D - 1][:, HALF:S])
                finish(1, spent[:, 0:HALF])
                finish(2, spent[:, HALF:S])
                finish(3, sq1[:, 1, HALF:HALF + P])
        finish(last, sq1[:, 1, HALF + P:S])
